import numpy as np
import ml_dtypes


def mxq(x, axis, fmt="e4m3"):
    dtype, down = {"e4m3": (ml_dtypes.float8_e4m3fn, 7), "e5m2": (ml_dtypes.float8_e5m2, 14)}[fmt]
    v = np.moveaxis(np.asarray(x, np.float32).astype(ml_dtypes.bfloat16).astype(np.float64), axis, -1)
    blocks = v.reshape(v.shape[:-1] + (-1, 32))
    amax = np.abs(blocks).max(-1, keepdims=True)
    byte = np.maximum(np.where(amax > 0, np.frexp(amax)[1] - 1 + 127, 0) - down, 1)
    scale = np.exp2(byte - 127.0)
    codes = (blocks / scale).astype(np.float32).astype(dtype).astype(np.float64)
    return np.moveaxis((codes * scale).reshape(v.shape), -1, axis)


WIDE = False


def mx_kscale(k):
    if not WIDE:
        return np.ones(k)
    levels = np.array([10, -10, 5, -5, 0])
    if k % 512:
        return np.exp2(np.random.permutation(np.resize(levels, k // 32))).repeat(32)
    a = np.empty((k // 512, 16))
    for p in range(k // 512):
        a[p, :8] = np.random.permutation(np.resize(levels, 8))
        for g in range(8):
            far = levels[np.abs(levels - a[p, g]) >= 10]
            a[p, g + 8] = far[np.random.randint(len(far))]
    return np.exp2(a.ravel()).repeat(32)


def f64(x):
    return np.asarray(x).astype(np.float64)


def striped(idx):
    return np.tile(idx.reshape(-1, 16).T, (8, 1)).astype(np.uint16)


def unstriped(offs):
    return offs[:16].T.reshape(-1).astype(np.int64)


def striped8(idx):
    return np.concatenate([x.reshape(-1, 16).T for x in idx]).astype(np.uint16)


def runs(offs, k):
    lists = np.stack([offs[16 * r : 16 * r + 16].T.reshape(-1) for r in range(8)]).astype(np.int64)
    return lists[np.arange(k) % 512 // 64]


def pack_weight(w):
    k, n = w.shape
    w = f64(np.asarray(w, np.float32).astype(ml_dtypes.bfloat16)).reshape(k // 32, 32, n)
    amax = np.abs(w).max(1)
    byte = np.clip(np.where(amax > 0, np.frexp(amax)[1] - 1 + 127 - 7, 1), 1, 254)
    scaled = (w * np.exp2(127.0 - byte)[:, None, :]).reshape(k, n).astype(np.float32)
    words = np.ascontiguousarray(scaled.reshape(k // 512, 128, 4, n).transpose(0, 1, 3, 2)).astype(ml_dtypes.float8_e4m3fn).view(np.uint8)
    return words, np.ascontiguousarray(byte.astype(np.uint8).reshape(k // 512, 16, n))


def unpack_weight(words, scales):
    g, p, n, _ = words.shape
    vals = np.ascontiguousarray(words).view(ml_dtypes.float8_e4m3fn).astype(np.float64) * np.repeat(np.exp2(scales.astype(np.float64) - 127.0), 8, axis=1)[..., None]
    return vals.transpose(0, 1, 3, 2).reshape(g * 512, n)


def sigmoid(v):
    return 1.0 / (1.0 + np.exp(-np.maximum(v, -700.0)))


K, T, S, N, H = 512, 2048, 512, 512, 512


def setup_inputs():
    n = np.random.standard_normal
    s = mx_kscale(K)[:, None]
    u = mx_kscale(H)
    packed_xT = pack_weight(n((K, T)) * s)
    return {
        "x_words": packed_xT[0],
        "x_scales": packed_xT[1],
        "w1": (n((K, H)) / np.sqrt(K) / s).astype(np.float32),
        "gn": (np.random.uniform(0.5, 1.5, (H, 1)) * u[:, None]).astype(np.float32),
        "w2": (n((H, N)) / np.sqrt(H) / u[:, None]).astype(np.float32),
        "offs": striped(np.random.permutation(T)[:S]),
        "n1": striped8(np.stack([np.random.permutation(S) for _ in range(8)])),
        "n2": striped8(np.stack([np.random.permutation(S) for _ in range(8)])),
        "n3": striped8(np.stack([np.random.permutation(S) for _ in range(8)])),
    }


def reference(x_words, x_scales, w1, gn, w2, offs, n1, n2, n3):
    xq = unpack_weight(x_words, x_scales)[:, unstriped(offs)]
    y = mxq(f64(w1), 0, "e4m3").T @ xq
    st = y * (sigmoid(y[np.arange(H)[:, None], runs(n1, H)]))
    z = f64(gn) * (np.maximum(st, st[np.arange(H)[:, None], runs(n1, H)]))
    h = mxq(f64(w2), 0, "e4m3").T @ mxq(z, 0, "e4m3")
    return 0.75 * (h * (y[np.arange(H)[:, None], runs(n3, H)]) - ((h[np.arange(N)[:, None], runs(n2, N)]) * y))

@@ -1,0 +1,181 @@
+from contextlib import ExitStack
+
+import concourse.mybir as mybir
+
+K, T, S, N, H = 512, 2048, 512, 512, 512
+FLOPS = 2 * K * H * S + 2 * H * N * S
+
+F32 = mybir.dt.float32
+BF16 = mybir.dt.bfloat16
+I32 = mybir.dt.int32
+U32 = mybir.dt.uint32
+U16 = mybir.dt.uint16
+U8 = mybir.dt.uint8
+FP8X4 = mybir.dt.float8_e4m3fn_x4
+ALU = mybir.AluOpType
+ACT = mybir.ActivationFunctionType
+
+P = 128
+PACK = 4
+
+
+def deal_views(raw, dealt, m_raw, m_dealt):
+    src = raw[:].rearrange("p j (m t) -> p m j t", t=PACK)[:, m_raw, :, :]
+    dst = dealt[:].rearrange("p (t m j) -> p m j t", t=PACK, j=PACK)[:, m_dealt, :, :]
+    return dst, src
+
+
+def tile_picked_skipcrossbtwicp_none_p_kernel(tc, x_words, x_scales, w1, gn, w2, offs, n1, n2, n3, out):
+    nc = tc.nc
+    with ExitStack() as ctx:
+        keep = ctx.enter_context(tc.tile_pool(name="keep", bufs=1))
+        psum = ctx.enter_context(tc.psum_pool(name="psum", bufs=1))
+
+        offs_sb = keep.tile([P, S // 16], U16, name="offs_sb")
+        n1_sb = keep.tile([P, S // 16], U16, name="n1_sb")
+        n2_sb = keep.tile([P, S // 16], U16, name="n2_sb")
+        n3_sb = keep.tile([P, S // 16], U16, name="n3_sb")
+        table_words = keep.tile([P, T], U32, name="table_words", align_bytes=64)
+        table_scales = keep.tile([P, T], U8, name="table_scales", align_bytes=64)
+        w1_raw = [keep.tile([P, PACK, H // 2], F32, name=f"w1_raw{i}", tag=f"raw{i}") for i in range(2)]
+        gain = keep.tile([P, PACK], F32, name="gain")
+        y_win = [keep.tile([P, 2 * S], F32, name=f"y_win{t}") for t in range(PACK)]
+        st_win = [keep.tile([P, 2 * S], F32, name=f"st_win{t}") for t in range(PACK)]
+        warm = keep.tile([P, 2], F32, name="warm")
+
+        nc.vector.memset(table_scales[:].bitcast(I32), 0)
+        nc.vector.memset(warm[:, 0:1], 0.0)
+        nc.sync.dma_start(offs_sb[:], offs)
+        nc.sync.dma_start(n1_sb[:], n1)
+        nc.sync.dma_start(n3_sb[:], n3)
+        nc.sync.dma_start(n2_sb[:], n2)
+        nc.sync.dma_start(out=table_words[:].bitcast(I32), in_=x_words[0].rearrange("p n t -> p (n t)").bitcast(I32))
+        for q in range(4):
+            nc.scalar.dma_start(out=table_scales[32 * q : 32 * q + 4, :].bitcast(I32), in_=x_scales[0, 4 * q : 4 * q + 4, :].bitcast(I32))
+        w1_rows = w1.rearrange("(p j) c -> p j c", j=PACK)
+        for i in range(2):
+            nc.sync.dma_start(out=w1_raw[i][:], in_=w1_rows[:, :, i * (H // 2) : (i + 1) * (H // 2)])
+        nc.gpsimd.dma_start(out=gain[:], in_=gn.rearrange("(p t) o -> p (t o)", t=PACK))
+        nc.scalar.activation(warm[:, 1:2], warm[:, 0:1], ACT.Sigmoid)
+        for t in range(PACK):
+            nc.vector.memset(y_win[t][:, S:], 0.0)
+
+        x_codes = keep.tile([P, S], U32, name="x_codes", align_bytes=64)
+        x_plane = keep.tile([P, S], U8, name="x_plane", align_bytes=64)
+        nc.vector.tensor_copy(x_plane[:], table_scales[:].indirect(offs_sb[:]))
+        nc.vector.tensor_copy(x_codes[:], table_words[:].indirect(offs_sb[:]))
+
+        w1_dealt = keep.tile([P, PACK * H], BF16, name="w1_dealt", align_bytes=64)
+        nc.vector.tensor_copy(*deal_views(w1_raw[0], w1_dealt, slice(0, 64), slice(0, 64)))
+        nc.vector.tensor_copy(*deal_views(w1_raw[1], w1_dealt, slice(0, 44), slice(64, 108)))
+        nc.scalar.copy(*deal_views(w1_raw[1], w1_dealt, slice(44, 64), slice(108, 128)))
+        w2_raw = [keep.tile([P, PACK, N // 2], F32, name=f"w2_raw{i}", tag=f"raw{i}") for i in range(2)]
+        w2_rows = w2.rearrange("(p j) c -> p j c", j=PACK)
+        for i in range(2):
+            nc.sync.dma_start(out=w2_raw[i][:], in_=w2_rows[:, :, i * (N // 2) : (i + 1) * (N // 2)])
+        w1_codes = keep.tile([P, H], U32, name="w1_codes", align_bytes=64)
+        w1_plane = keep.tile([P, H], U8, name="w1_plane", align_bytes=64)
+        for a, b in ((0, 128), (128, 256), (256, 512)):
+            nc.vector.quantize_mx(out=w1_codes[:, a:b].bitcast(FP8X4), scales=w1_plane[:, a:b], in_=w1_dealt[:, PACK * a : PACK * b])
+
+        y_ps = [psum.tile([P, S], F32, name=f"y_ps{t}") for t in range(PACK)]
+        for t in range(PACK):
+            cols = slice(t * P, (t + 1) * P)
+            nc.tensor.matmul_mx(out=y_ps[t][:], lhsT=w1_codes[:, cols].bitcast(FP8X4), lhsT_scale=w1_plane[:, cols],
+                                rhs=x_codes[:].bitcast(FP8X4), rhs_scale=x_plane[:], start=True, stop=True)
+
+        def sig(t):
+            nc.scalar.activation(st_win[t][:, S:], y_win[t][:].indirect(n1_sb[:]), ACT.Sigmoid)
+
+        nc.scalar.copy(y_win[0][:, :S], y_ps[0][:])
+        nc.vector.tensor_copy(y_win[1][:, :S], y_ps[1][:])
+        nc.vector.tensor_copy(y_win[2][:, :S], y_ps[2][:])
+        sig(0)
+        sig(1)
+        nc.scalar.copy(y_win[3][:, :S], y_ps[3][:])
+        sig(2)
+        sig(3)
+
+        far = [keep.tile([P, S], F32, name=f"far{t}") for t in range(PACK)]
+        z_rows = keep.tile([P, PACK, S], BF16, name="z_rows")
+
+        def gate(t):
+            nc.vector.tensor_tensor(st_win[t][:, :S], y_ps[t][:], st_win[t][:, S:], ALU.mult)
+
+        def fetch(t):
+            nc.vector.tensor_copy(far[t][:], st_win[t][:].indirect(n1_sb[:]))
+
+        def larger(t):
+            nc.vector.tensor_tensor(far[t][:], far[t][:], st_win[t][:, :S], ALU.max)
+
+        w2_dealt = keep.tile([P, PACK * N], BF16, name="w2_dealt", align_bytes=64)
+        w2_codes = keep.tile([P, N], U32, name="w2_codes", align_bytes=64)
+        w2_plane = keep.tile([P, N], U8, name="w2_plane", align_bytes=64)
+
+        def deal_w2(i):
+            nc.scalar.copy(*deal_views(w2_raw[i // 2], w2_dealt, slice(32 * (i % 2), 32 * (i % 2 + 1)), slice(32 * i, 32 * (i + 1))))
+
+        gate(0)
+        fetch(0)
+        for t in range(1, PACK):
+            gate(t)
+            larger(t - 1)
+            nc.scalar.activation(z_rows[:, t - 1, :], far[t - 1][:], ACT.Copy, scale=gain[:, t - 1 : t])
+            fetch(t)
+        for i in range(4):
+            deal_w2(i)
+        nc.vector.quantize_mx(out=w2_codes[:].bitcast(FP8X4), scales=w2_plane[:], in_=w2_dealt[:])
+        halves = [slice(0, S // 2), slice(S // 2, S)]
+        for c in halves:
+            nc.vector.tensor_tensor(far[3][:, c], far[3][:, c], st_win[3][:, c], ALU.max)
+        for c in halves:
+            nc.vector.tensor_scalar(z_rows[:, 3, c], far[3][:, c], gain[:, 3:4], None, ALU.mult)
+
+        z_woven = [keep.tile([P, PACK * S // 2], BF16, name=f"z_woven{i}", tag=f"z_woven{i}", align_bytes=64) for i in range(2)]
+        z_codes = keep.tile([P, S], U32, name="z_codes", align_bytes=64)
+        z_plane = keep.tile([P, S], U8, name="z_plane", align_bytes=64)
+        for i in range(2):
+            src = z_rows[:, :, halves[i]].rearrange("p t (c i) -> p c t i", i=4)
+            dst = z_woven[i][:].rearrange("p (c i t) -> p c t i", i=4, t=PACK)
+            nc.vector.tensor_copy(dst[:, 0:40], src[:, 0:40])
+            nc.scalar.copy(dst[:, 40:64], src[:, 40:64])
+        for i in range(2):
+            nc.vector.quantize_mx(out=z_codes[:, halves[i]].bitcast(FP8X4), scales=z_plane[:, halves[i]], in_=z_woven[i][:])
+
+        h_ps = [psum.tile([P, S], F32, name=f"h_ps{t}") for t in range(PACK)]
+
+        def second_product(t, c):
+            cols = slice(t * P, (t + 1) * P)
+            nc.tensor.matmul_mx(out=h_ps[t][:, c], lhsT=w2_codes[:, cols].bitcast(FP8X4), lhsT_scale=w2_plane[:, cols],
+                                rhs=z_codes[:, c].bitcast(FP8X4), rhs_scale=z_plane[:, c], start=True, stop=True)
+
+        for t in range(PACK):
+            for c in halves:
+                second_product(t, c)
+            nc.scalar.activation(st_win[t][:, :S], h_ps[t][:], ACT.Copy, scale=0.75)
+
+        y_far = keep.tile([P, S], F32, name="y_far", tag="z_woven1", align_bytes=64)
+        nc.vector.tensor_copy(y_far[:], y_win[3][:].indirect(n3_sb[:]))
+
+        out_rows = out.rearrange("(p t) s -> p t s", t=PACK)
+        first = [keep.tile([P, S], F32, name=f"first{t}") for t in range(PACK)]
+
+        def first_term(t):
+            if t == 3:
+                nc.vector.tensor_tensor(first[t][:], y_far[:], st_win[t][:, :S], ALU.mult)
+            else:
+                nc.vector.tensor_tensor(first[t][:], y_win[t][:].indirect(n3_sb[:]), st_win[t][:, :S], ALU.mult)
+
+        def second_term(t):
+            nc.vector.tensor_tensor(far[t][:], st_win[t][:].indirect(n2_sb[:]), y_win[t][:, :S], ALU.mult)
+
+        def finish(t):
+            nc.vector.tensor_tensor(first[t][:], first[t][:], far[t][:], ALU.subtract)
+            nc.sync.dma_start(out=out_rows[:, t, :], in_=first[t][:])
+
+        for t in range(PACK):
+            second_term(t)
+            if t > 0:
+                finish(t - 1)
+            first_term(t)
+        finish(3)

@@ -1,6 +1,7 @@
 from contextlib import ExitStack
 
 import concourse.mybir as mybir
+from concourse.masks import make_identity
 
 K, T, S, N, H = 512, 2048, 512, 512, 512
 FLOPS = 2 * K * H * S + 2 * H * N * S
@@ -30,18 +31,22 @@ def tile_picked_skipcrossbtwicp_none_p_kernel(tc, x_words, x_scales, w1, gn, w2,
     with ExitStack() as ctx:
         keep = ctx.enter_context(tc.tile_pool(name="keep", bufs=1))
         psum = ctx.enter_context(tc.psum_pool(name="psum", bufs=1))
+        HALF = S // 2
+        halves = [slice(0, HALF), slice(HALF, S)]
+        list_halves = [slice(0, HALF // 16), slice(HALF // 16, S // 16)]
 
         offs_sb = keep.tile([P, S // 16], U16, name="offs_sb")
         n1_sb = keep.tile([P, S // 16], U16, name="n1_sb")
         n2_sb = keep.tile([P, S // 16], U16, name="n2_sb")
         n3_sb = keep.tile([P, S // 16], U16, name="n3_sb")
         table_words = keep.tile([P, T], U32, name="table_words", align_bytes=64)
-        table_scales = keep.tile([P, T], U8, name="table_scales", align_bytes=64)
+        table_scales = keep.tile([P, T], U8, name="table_scales", tag="scales_then_codes", align_bytes=64)
         w1_raw = [keep.tile([P, PACK, H // 2], F32, name=f"w1_raw{i}", tag=f"raw{i}") for i in range(2)]
         gain = keep.tile([P, PACK], F32, name="gain")
         y_win = [keep.tile([P, 2 * S], F32, name=f"y_win{t}") for t in range(PACK)]
         st_win = [keep.tile([P, 2 * S], F32, name=f"st_win{t}") for t in range(PACK)]
         warm = keep.tile([P, 2], F32, name="warm")
+        ident = keep.tile([P, P], F32, name="ident")
 
         nc.vector.memset(table_scales[:].bitcast(I32), 0)
         nc.vector.memset(warm[:, 0:1], 0.0)
@@ -49,133 +54,165 @@ def tile_picked_skipcrossbtwicp_none_p_kernel(tc, x_words, x_scales, w1, gn, w2,
         nc.sync.dma_start(n1_sb[:], n1)
         nc.sync.dma_start(n3_sb[:], n3)
         nc.sync.dma_start(n2_sb[:], n2)
-        nc.sync.dma_start(out=table_words[:].bitcast(I32), in_=x_words[0].rearrange("p n t -> p (n t)").bitcast(I32))
         for q in range(4):
             nc.scalar.dma_start(out=table_scales[32 * q : 32 * q + 4, :].bitcast(I32), in_=x_scales[0, 4 * q : 4 * q + 4, :].bitcast(I32))
         w1_rows = w1.rearrange("(p j) c -> p j c", j=PACK)
         for i in range(2):
             nc.sync.dma_start(out=w1_raw[i][:], in_=w1_rows[:, :, i * (H // 2) : (i + 1) * (H // 2)])
+        nc.sync.dma_start(out=table_words[:].bitcast(I32), in_=x_words[0].rearrange("p n t -> p (n t)").bitcast(I32))
         nc.gpsimd.dma_start(out=gain[:], in_=gn.rearrange("(p t) o -> p (t o)", t=PACK))
         nc.scalar.activation(warm[:, 1:2], warm[:, 0:1], ACT.Sigmoid)
         for t in range(PACK):
             nc.vector.memset(y_win[t][:, S:], 0.0)
-
-        x_codes = keep.tile([P, S], U32, name="x_codes", align_bytes=64)
-        x_plane = keep.tile([P, S], U8, name="x_plane", align_bytes=64)
-        nc.vector.tensor_copy(x_plane[:], table_scales[:].indirect(offs_sb[:]))
-        nc.vector.tensor_copy(x_codes[:], table_words[:].indirect(offs_sb[:]))
+        make_identity(nc, ident[:])
 
         w1_dealt = keep.tile([P, PACK * H], BF16, name="w1_dealt", align_bytes=64)
         nc.vector.tensor_copy(*deal_views(w1_raw[0], w1_dealt, slice(0, 64), slice(0, 64)))
-        nc.vector.tensor_copy(*deal_views(w1_raw[1], w1_dealt, slice(0, 44), slice(64, 108)))
-        nc.scalar.copy(*deal_views(w1_raw[1], w1_dealt, slice(44, 64), slice(108, 128)))
+        nc.vector.tensor_copy(*deal_views(w1_raw[1], w1_dealt, slice(0, 32), slice(64, 96)))
+        nc.scalar.copy(*deal_views(w1_raw[1], w1_dealt, slice(32, 64), slice(96, 128)))
+
+        x_plane = keep.tile([P, S], U8, name="x_plane", align_bytes=64)
+        nc.vector.tensor_copy(x_plane[:], table_scales[:].indirect(offs_sb[:]))
+        w1_codes = keep.tile([P, H], U32, name="w1_codes", align_bytes=64)
+        w1_plane = keep.tile([P, H], U8, name="w1_plane", align_bytes=64)
+        nc.vector.quantize_mx(out=w1_codes[:].bitcast(FP8X4), scales=w1_plane[:], in_=w1_dealt[:])
+        x_codes = keep.tile([P, S], U32, name="x_codes", tag="scales_then_codes", align_bytes=64)
+        for i in range(2):
+            nc.vector.tensor_copy(x_codes[:, halves[i]], table_words[:].indirect(offs_sb[:, list_halves[i]]))
+
         w2_raw = [keep.tile([P, PACK, N // 2], F32, name=f"w2_raw{i}", tag=f"raw{i}") for i in range(2)]
         w2_rows = w2.rearrange("(p j) c -> p j c", j=PACK)
         for i in range(2):
             nc.sync.dma_start(out=w2_raw[i][:], in_=w2_rows[:, :, i * (N // 2) : (i + 1) * (N // 2)])
-        w1_codes = keep.tile([P, H], U32, name="w1_codes", align_bytes=64)
-        w1_plane = keep.tile([P, H], U8, name="w1_plane", align_bytes=64)
-        for a, b in ((0, 128), (128, 256), (256, 512)):
-            nc.vector.quantize_mx(out=w1_codes[:, a:b].bitcast(FP8X4), scales=w1_plane[:, a:b], in_=w1_dealt[:, PACK * a : PACK * b])
 
-        y_ps = [psum.tile([P, S], F32, name=f"y_ps{t}") for t in range(PACK)]
-        for t in range(PACK):
+        def product(dst, w_codes, w_plane, t, codes, plane, c):
             cols = slice(t * P, (t + 1) * P)
-            nc.tensor.matmul_mx(out=y_ps[t][:], lhsT=w1_codes[:, cols].bitcast(FP8X4), lhsT_scale=w1_plane[:, cols],
-                                rhs=x_codes[:].bitcast(FP8X4), rhs_scale=x_plane[:], start=True, stop=True)
+            nc.tensor.matmul_mx(out=dst, lhsT=w_codes[:, cols].bitcast(FP8X4), lhsT_scale=w_plane[:, cols],
+                                rhs=codes[:, c].bitcast(FP8X4), rhs_scale=plane[:, c], start=True, stop=True)
+
+        y0_ps = [psum.tile([P, HALF], F32, name=f"y0_ps{i}", tag=f"bank{i}") for i in range(2)]
+        y_ps = [None] + [psum.tile([P, S], F32, name=f"y_ps{t}", tag=f"bank{t + 1}") for t in range(1, PACK)]
+        for i in range(2):
+            product(y0_ps[i][:], w1_codes, w1_plane, 0, x_codes, x_plane, halves[i])
+            nc.scalar.copy(y_win[0][:, halves[i]], y0_ps[i][:])
+            product(y_ps[1][:, halves[i]], w1_codes, w1_plane, 1, x_codes, x_plane, halves[i])
+        for t in (2, 3):
+            product(y_ps[t][:], w1_codes, w1_plane, t, x_codes, x_plane, slice(0, S))
 
         def sig(t):
             nc.scalar.activation(st_win[t][:, S:], y_win[t][:].indirect(n1_sb[:]), ACT.Sigmoid)
 
-        nc.scalar.copy(y_win[0][:, :S], y_ps[0][:])
-        nc.vector.tensor_copy(y_win[1][:, :S], y_ps[1][:])
-        nc.vector.tensor_copy(y_win[2][:, :S], y_ps[2][:])
-        sig(0)
-        sig(1)
-        nc.scalar.copy(y_win[3][:, :S], y_ps[3][:])
-        sig(2)
-        sig(3)
-
-        far = [keep.tile([P, S], F32, name=f"far{t}") for t in range(PACK)]
-        z_rows = keep.tile([P, PACK, S], BF16, name="z_rows")
-
-        def gate(t):
-            nc.vector.tensor_tensor(st_win[t][:, :S], y_ps[t][:], st_win[t][:, S:], ALU.mult)
-
-        def fetch(t):
-            nc.vector.tensor_copy(far[t][:], st_win[t][:].indirect(n1_sb[:]))
-
-        def larger(t):
-            nc.vector.tensor_tensor(far[t][:], far[t][:], st_win[t][:, :S], ALU.max)
-
         w2_dealt = keep.tile([P, PACK * N], BF16, name="w2_dealt", align_bytes=64)
         w2_codes = keep.tile([P, N], U32, name="w2_codes", align_bytes=64)
         w2_plane = keep.tile([P, N], U8, name="w2_plane", align_bytes=64)
+        nc.vector.tensor_copy(*deal_views(w2_raw[0], w2_dealt, slice(0, 64), slice(0, 64)))
+        nc.vector.tensor_copy(y_win[1][:, :S], y_ps[1][:])
+        nc.vector.tensor_copy(*deal_views(w2_raw[1], w2_dealt, slice(0, 64), slice(64, 128)))
+        for i in range(2):
+            nc.scalar.activation(st_win[0][:, S + i * HALF : S + (i + 1) * HALF], y_win[0][:].indirect(n1_sb[:, list_halves[i]]), ACT.Sigmoid)
+        sig(1)
+        for t in (2, 3):
+            nc.scalar.copy(y_win[t][:, :S], y_ps[t][:])
+            sig(t)
 
-        def deal_w2(i):
-            nc.scalar.copy(*deal_views(w2_raw[i // 2], w2_dealt, slice(32 * (i % 2), 32 * (i % 2 + 1)), slice(32 * i, 32 * (i + 1))))
+        y_minus = [None] + [keep.tile([P, S], F32, name=f"y_minus{t}") for t in (1, 2)]
+        for t in (1, 2):
+            nc.scalar.activation(y_minus[t][:], y_win[t][:, :S], ACT.Copy, scale=-1.0)
+        far = [keep.tile([P, S], F32, name=f"far{t}") for t in range(PACK)]
+        z_pairs = [keep.tile([P, 2, HALF, 2], BF16, name=f"z_pairs{i}") for i in range(2)]
 
-        gate(0)
-        fetch(0)
-        for t in range(1, PACK):
-            gate(t)
-            larger(t - 1)
-            nc.scalar.activation(z_rows[:, t - 1, :], far[t - 1][:], ACT.Copy, scale=gain[:, t - 1 : t])
-            fetch(t)
-        for i in range(4):
-            deal_w2(i)
+        def gate(t):
+            nc.vector.tensor_tensor(st_win[t][:, :S], y_win[t][:, :S], st_win[t][:, S:], ALU.mult)
+
+        def larger(t, c):
+            nc.vector.tensor_tensor(far[t][:, c], far[t][:, c], st_win[t][:, c], ALU.max)
+
+        def scale(t, i):
+            nc.scalar.activation(z_pairs[i][:, t // 2, :, t % 2], far[t][:, halves[i]], ACT.Copy, scale=gain[:, t : t + 1])
+
+        for i in range(2):
+            nc.vector.tensor_tensor(st_win[0][:, halves[i]], y_win[0][:, halves[i]], st_win[0][:, S + i * HALF : S + (i + 1) * HALF], ALU.mult)
         nc.vector.quantize_mx(out=w2_codes[:].bitcast(FP8X4), scales=w2_plane[:], in_=w2_dealt[:])
-        halves = [slice(0, S // 2), slice(S // 2, S)]
-        for c in halves:
-            nc.vector.tensor_tensor(far[3][:, c], far[3][:, c], st_win[3][:, c], ALU.max)
-        for c in halves:
-            nc.vector.tensor_scalar(z_rows[:, 3, c], far[3][:, c], gain[:, 3:4], None, ALU.mult)
+        for t in range(PACK - 1):
+            nc.vector.tensor_copy(far[t][:], st_win[t][:].indirect(n1_sb[:]))
+            gate(t + 1)
+            larger(t, slice(0, S))
+            for i in range(2):
+                scale(t, i)
+        for i in range(2):
+            nc.vector.tensor_copy(far[3][:, halves[i]], st_win[3][:].indirect(n1_sb[:, list_halves[i]]))
+        for i in range(2):
+            larger(3, halves[i])
+            scale(3, i)
 
-        z_woven = [keep.tile([P, PACK * S // 2], BF16, name=f"z_woven{i}", tag=f"z_woven{i}", align_bytes=64) for i in range(2)]
+        y_far0 = st_win[3][:, S : S + HALF]
+        nc.vector.tensor_copy(y_far0, y_win[0][:].indirect(n3_sb[:, list_halves[0]]))
+
+        z_woven = [keep.tile([P, PACK * HALF], BF16, name=f"z_woven{i}", tag=f"z_woven{i}", align_bytes=64) for i in range(2)]
         z_codes = keep.tile([P, S], U32, name="z_codes", align_bytes=64)
         z_plane = keep.tile([P, S], U8, name="z_plane", align_bytes=64)
         for i in range(2):
-            src = z_rows[:, :, halves[i]].rearrange("p t (c i) -> p c t i", i=4)
-            dst = z_woven[i][:].rearrange("p (c i t) -> p c t i", i=4, t=PACK)
-            nc.vector.tensor_copy(dst[:, 0:40], src[:, 0:40])
-            nc.scalar.copy(dst[:, 40:64], src[:, 40:64])
+            src = z_pairs[i][:].rearrange("p u s e -> p (u s e)").bitcast(F32).rearrange("p (u s) -> p s u", u=2)
+            dst = z_woven[i][:].bitcast(F32).rearrange("p (s u) -> p s u", u=2)
+            nc.vector.tensor_copy(dst, src)
         for i in range(2):
             nc.vector.quantize_mx(out=z_codes[:, halves[i]].bitcast(FP8X4), scales=z_plane[:, halves[i]], in_=z_woven[i][:])
+        y_far1 = keep.tile([P, HALF], F32, name="y_far1", tag="z_woven1", align_bytes=64)
+        nc.vector.tensor_copy(y_far1[:], y_win[0][:].indirect(n3_sb[:, list_halves[1]]))
+        y_far = [y_far0, y_far1[:]]
 
-        h_ps = [psum.tile([P, S], F32, name=f"h_ps{t}") for t in range(PACK)]
+        first = [keep.tile([P, S], F32, name=f"first{t}") for t in range(PACK)]
+        h0_ps = [psum.tile([P, HALF], F32, name=f"h0_ps{i}", tag=f"bank{5 + i}") for i in range(2)]
+        h_ps = [None] + [psum.tile([P, S], F32, name=f"h_ps{t}", tag=f"bank{(6 + t) % 8}") for t in range(1, PACK)]
+        for i in range(2):
+            product(h0_ps[i][:], w2_codes, w2_plane, 0, z_codes, z_plane, halves[i])
+            nc.scalar.activation(st_win[0][:, halves[i]], h0_ps[i][:], ACT.Copy, scale=0.75)
+            nc.vector.scalar_tensor_tensor(first[0][:, halves[i]], h0_ps[i][:], -0.75, y_far[i], ALU.mult, ALU.mult)
+            product(h_ps[1][:, halves[i]], w2_codes, w2_plane, 1, z_codes, z_plane, halves[i])
+        for t in (2, 3):
+            product(h_ps[t][:], w2_codes, w2_plane, t, z_codes, z_plane, slice(0, S))
 
-        def second_product(t, c):
-            cols = slice(t * P, (t + 1) * P)
-            nc.tensor.matmul_mx(out=h_ps[t][:, c], lhsT=w2_codes[:, cols].bitcast(FP8X4), lhsT_scale=w2_plane[:, cols],
-                                rhs=z_codes[:, c].bitcast(FP8X4), rhs_scale=z_plane[:, c], start=True, stop=True)
-
-        for t in range(PACK):
-            for c in halves:
-                second_product(t, c)
+        def leave_bank(t):
             nc.scalar.activation(st_win[t][:, :S], h_ps[t][:], ACT.Copy, scale=0.75)
 
-        y_far = keep.tile([P, S], F32, name="y_far", tag="z_woven1", align_bytes=64)
-        nc.vector.tensor_copy(y_far[:], y_win[3][:].indirect(n3_sb[:]))
+        leave_bank(1)
 
         out_rows = out.rearrange("(p t) s -> p t s", t=PACK)
-        first = [keep.tile([P, S], F32, name=f"first{t}") for t in range(PACK)]
 
-        def first_term(t):
-            if t == 3:
-                nc.vector.tensor_tensor(first[t][:], y_far[:], st_win[t][:, :S], ALU.mult)
-            else:
-                nc.vector.tensor_tensor(first[t][:], y_win[t][:].indirect(n3_sb[:]), st_win[t][:, :S], ALU.mult)
+        def add_on_tensor(t, terms, c, banks):
+            width = c.stop - c.start
+            blocks = [slice(b * P, (b + 1) * P) for b in range(width // P)]
+            turned_ps = psum.tile([P, width], F32, name=f"turned_ps{banks[1]}", tag=f"bank{banks[0]}")
+            for k, term in enumerate(terms):
+                for b, block in enumerate(blocks):
+                    nc.tensor.matmul(turned_ps[:, block], lhsT=term[:, c][:, block], rhs=ident[:], is_transpose=True,
+                                     start=(k == 0 and b == 0), stop=(k == 1 and b == len(blocks) - 1))
+            turned = keep.tile([P, width], F32, name=f"turned{banks[1]}")
+            nc.scalar.copy(turned[:], turned_ps[:])
+            back_ps = psum.tile([P, width], F32, name=f"back_ps{banks[1]}", tag=f"bank{banks[1]}")
+            for block in blocks:
+                nc.tensor.transpose(back_ps[:, block], turned[:, block], ident[:])
+            done = keep.tile([P, width], F32, name=f"done{banks[1]}")
+            nc.scalar.activation(done[:], back_ps[:], ACT.Copy, scale=-1.0 if t == 0 else 1.0)
+            nc.scalar.dma_start(out=out_rows[:, t, c], in_=done[:])
 
-        def second_term(t):
-            nc.vector.tensor_tensor(far[t][:], st_win[t][:].indirect(n2_sb[:]), y_win[t][:, :S], ALU.mult)
-
-        def finish(t):
-            nc.vector.tensor_tensor(first[t][:], first[t][:], far[t][:], ALU.subtract)
-            nc.sync.dma_start(out=out_rows[:, t, :], in_=first[t][:])
-
-        for t in range(PACK):
-            second_term(t)
-            if t > 0:
-                finish(t - 1)
-            first_term(t)
-        finish(3)
+        whole = slice(0, S)
+        nc.vector.tensor_tensor(far[0][:], st_win[0][:].indirect(n2_sb[:]), y_win[0][:, :S], ALU.mult)
+        add_on_tensor(0, (first[0], far[0]), whole, (2, 4))
+        leave_bank(2)
+        nc.vector.tensor_tensor(far[1][:], st_win[1][:].indirect(n2_sb[:]), y_minus[1][:], ALU.mult)
+        nc.vector.tensor_tensor(first[1][:], y_win[1][:].indirect(n3_sb[:]), st_win[1][:, :S], ALU.mult)
+        add_on_tensor(1, (far[1], first[1]), whole, (2, 6))
+        leave_bank(3)
+        nc.vector.tensor_tensor(far[2][:], st_win[2][:].indirect(n2_sb[:]), y_minus[2][:], ALU.mult)
+        for i in range(2):
+            nc.vector.tensor_tensor(first[2][:, halves[i]], y_win[2][:].indirect(n3_sb[:, list_halves[i]]), st_win[2][:, halves[i]], ALU.mult)
+        add_on_tensor(2, (far[2], first[2]), halves[0], (2, 7))
+        nc.vector.tensor_tensor(first[3][:], y_win[3][:].indirect(n3_sb[:]), st_win[3][:, :S], ALU.mult)
+        nc.vector.tensor_tensor(first[2][:, halves[1]], first[2][:, halves[1]], far[2][:, halves[1]], ALU.add)
+        nc.sync.dma_start(out=out_rows[:, 2, halves[1]], in_=first[2][:, halves[1]])
+        for i in range(2):
+            nc.vector.tensor_tensor(far[3][:, halves[i]], st_win[3][:].indirect(n2_sb[:, list_halves[i]]), y_win[3][:, halves[i]], ALU.mult)
+        for c in halves:
+            nc.vector.tensor_tensor(first[3][:, c], first[3][:, c], far[3][:, c], ALU.subtract)
+            nc.sync.dma_start(out=out_rows[:, 3, c], in_=first[3][:, c])

@@ -50,16 +50,16 @@ def tile_picked_skipcrossbtwicp_none_p_kernel(tc, x_words, x_scales, w1, gn, w2,
 
         nc.vector.memset(table_scales[:].bitcast(I32), 0)
         nc.vector.memset(warm[:, 0:1], 0.0)
+        w1_rows = w1.rearrange("(p j) c -> p j c", j=PACK)
+        nc.sync.dma_start(out=w1_raw[0][:], in_=w1_rows[:, :, : H // 2])
+        for q in range(4):
+            nc.sync.dma_start(out=table_scales[32 * q : 32 * q + 4, :].bitcast(I32), in_=x_scales[0, 4 * q : 4 * q + 4, :].bitcast(I32))
         nc.sync.dma_start(offs_sb[:], offs)
+        nc.sync.dma_start(out=w1_raw[1][:], in_=w1_rows[:, :, H // 2 :])
+        nc.sync.dma_start(out=table_words[:].bitcast(I32), in_=x_words[0].rearrange("p n t -> p (n t)").bitcast(I32))
         nc.sync.dma_start(n1_sb[:], n1)
         nc.sync.dma_start(n3_sb[:], n3)
         nc.sync.dma_start(n2_sb[:], n2)
-        for q in range(4):
-            nc.scalar.dma_start(out=table_scales[32 * q : 32 * q + 4, :].bitcast(I32), in_=x_scales[0, 4 * q : 4 * q + 4, :].bitcast(I32))
-        w1_rows = w1.rearrange("(p j) c -> p j c", j=PACK)
-        for i in range(2):
-            nc.sync.dma_start(out=w1_raw[i][:], in_=w1_rows[:, :, i * (H // 2) : (i + 1) * (H // 2)])
-        nc.sync.dma_start(out=table_words[:].bitcast(I32), in_=x_words[0].rearrange("p n t -> p (n t)").bitcast(I32))
         nc.gpsimd.dma_start(out=gain[:], in_=gn.rearrange("(p t) o -> p (t o)", t=PACK))
         nc.scalar.activation(warm[:, 1:2], warm[:, 0:1], ACT.Sigmoid)
         for t in range(PACK):
@@ -91,13 +91,11 @@ def tile_picked_skipcrossbtwicp_none_p_kernel(tc, x_words, x_scales, w1, gn, w2,
                                 rhs=codes[:, c].bitcast(FP8X4), rhs_scale=plane[:, c], start=True, stop=True)
 
         y0_ps = [psum.tile([P, HALF], F32, name=f"y0_ps{i}", tag=f"bank{i}") for i in range(2)]
-        y_ps = [None] + [psum.tile([P, S], F32, name=f"y_ps{t}", tag=f"bank{t + 1}") for t in range(1, PACK)]
+        y_ps = {1: psum.tile([P, S], F32, name="y_ps1", tag="bank2")}
         for i in range(2):
             product(y0_ps[i][:], w1_codes, w1_plane, 0, x_codes, x_plane, halves[i])
             nc.scalar.copy(y_win[0][:, halves[i]], y0_ps[i][:])
             product(y_ps[1][:, halves[i]], w1_codes, w1_plane, 1, x_codes, x_plane, halves[i])
-        for t in (2, 3):
-            product(y_ps[t][:], w1_codes, w1_plane, t, x_codes, x_plane, slice(0, S))
 
         def sig(t):
             nc.scalar.activation(st_win[t][:, S:], y_win[t][:].indirect(n1_sb[:]), ACT.Sigmoid)
@@ -112,14 +110,13 @@ def tile_picked_skipcrossbtwicp_none_p_kernel(tc, x_words, x_scales, w1, gn, w2,
             nc.scalar.activation(st_win[0][:, S + i * HALF : S + (i + 1) * HALF], y_win[0][:].indirect(n1_sb[:, list_halves[i]]), ACT.Sigmoid)
         sig(1)
         for t in (2, 3):
+            y_ps.setdefault(t, psum.tile([P, S], F32, name=f"y_ps{t}", tag=f"bank{t - 1}"))
+            product(y_ps[t][:], w1_codes, w1_plane, t, x_codes, x_plane, slice(0, S))
             nc.scalar.copy(y_win[t][:, :S], y_ps[t][:])
             sig(t)
 
-        y_minus = [None] + [keep.tile([P, S], F32, name=f"y_minus{t}") for t in (1, 2)]
-        for t in (1, 2):
-            nc.scalar.activation(y_minus[t][:], y_win[t][:, :S], ACT.Copy, scale=-1.0)
         far = [keep.tile([P, S], F32, name=f"far{t}") for t in range(PACK)]
-        z_pairs = [keep.tile([P, 2, HALF, 2], BF16, name=f"z_pairs{i}") for i in range(2)]
+        z_pairs = [keep.tile([P, 2, HALF, 2], BF16, name=f"z_pairs{i}", tag=f"z_pairs{i}") for i in range(2)]
 
         def gate(t):
             nc.vector.tensor_tensor(st_win[t][:, :S], y_win[t][:, :S], st_win[t][:, S:], ALU.mult)
@@ -177,6 +174,9 @@ def tile_picked_skipcrossbtwicp_none_p_kernel(tc, x_words, x_scales, w1, gn, w2,
 
         leave_bank(1)
 
+        y_minus = [None] + [keep.tile([P, S], F32, name=f"y_minus{t}", tag=f"z_pairs{t - 1}") for t in (1, 2)]
+        for t in (1, 2):
+            nc.scalar.activation(y_minus[t][:], y_win[t][:, :S], ACT.Copy, scale=-1.0)
         out_rows = out.rearrange("(p t) s -> p t s", t=PACK)
 
         def add_on_tensor(t, terms, c, banks):

@@ -64,6 +64,8 @@ def tile_picked_skipcrossbtwicp_none_p_kernel(tc, x_words, x_scales, w1, gn, w2,
         nc.scalar.activation(warm[:, 1:2], warm[:, 0:1], ACT.Sigmoid)
         for t in range(PACK):
             nc.vector.memset(y_win[t][:, S:], 0.0)
+        nc.vector.memset(st_win[0][:, S:], 0.0)
+        sigmoid0 = keep.tile([P, S], F32, name="sigmoid0")
         make_identity(nc, ident[:])
 
         w1_dealt = keep.tile([P, PACK * H], BF16, name="w1_dealt", align_bytes=64)
@@ -80,10 +82,9 @@ def tile_picked_skipcrossbtwicp_none_p_kernel(tc, x_words, x_scales, w1, gn, w2,
         for i in range(2):
             nc.vector.tensor_copy(x_codes[:, halves[i]], table_words[:].indirect(offs_sb[:, list_halves[i]]))
 
-        w2_raw = [keep.tile([P, PACK, N // 2], F32, name=f"w2_raw{i}", tag=f"raw{i}") for i in range(2)]
         w2_rows = w2.rearrange("(p j) c -> p j c", j=PACK)
-        for i in range(2):
-            nc.sync.dma_start(out=w2_raw[i][:], in_=w2_rows[:, :, i * (N // 2) : (i + 1) * (N // 2)])
+        w2_left = keep.tile([P, PACK, N // 2], F32, name="w2_left", tag="raw0")
+        nc.sync.dma_start(out=w2_left[:], in_=w2_rows[:, :, : N // 2])
 
         def product(dst, w_codes, w_plane, t, codes, plane, c):
             cols = slice(t * P, (t + 1) * P)
@@ -94,6 +95,7 @@ def tile_picked_skipcrossbtwicp_none_p_kernel(tc, x_words, x_scales, w1, gn, w2,
         y_ps = {1: psum.tile([P, S], F32, name="y_ps1", tag="bank2")}
         for i in range(2):
             product(y0_ps[i][:], w1_codes, w1_plane, 0, x_codes, x_plane, halves[i])
+            nc.scalar.activation(sigmoid0[:, halves[i]], y0_ps[i][:], ACT.Sigmoid)
             nc.scalar.copy(y_win[0][:, halves[i]], y0_ps[i][:])
             product(y_ps[1][:, halves[i]], w1_codes, w1_plane, 1, x_codes, x_plane, halves[i])
 
@@ -103,11 +105,8 @@ def tile_picked_skipcrossbtwicp_none_p_kernel(tc, x_words, x_scales, w1, gn, w2,
         w2_dealt = keep.tile([P, PACK * N], BF16, name="w2_dealt", align_bytes=64)
         w2_codes = keep.tile([P, N], U32, name="w2_codes", align_bytes=64)
         w2_plane = keep.tile([P, N], U8, name="w2_plane", align_bytes=64)
-        nc.vector.tensor_copy(*deal_views(w2_raw[0], w2_dealt, slice(0, 64), slice(0, 64)))
+        nc.vector.tensor_copy(*deal_views(w2_left, w2_dealt, slice(0, 64), slice(0, 64)))
         nc.vector.tensor_copy(y_win[1][:, :S], y_ps[1][:])
-        nc.vector.tensor_copy(*deal_views(w2_raw[1], w2_dealt, slice(0, 64), slice(64, 128)))
-        for i in range(2):
-            nc.scalar.activation(st_win[0][:, S + i * HALF : S + (i + 1) * HALF], y_win[0][:].indirect(n1_sb[:, list_halves[i]]), ACT.Sigmoid)
         sig(1)
         for t in (2, 3):
             y_ps.setdefault(t, psum.tile([P, S], F32, name=f"y_ps{t}", tag=f"bank{t - 1}"))
@@ -115,6 +114,10 @@ def tile_picked_skipcrossbtwicp_none_p_kernel(tc, x_words, x_scales, w1, gn, w2,
             nc.scalar.copy(y_win[t][:, :S], y_ps[t][:])
             sig(t)
 
+        w2_right = keep.tile([P, PACK, N // 2], F32, name="w2_right", tag="scales_then_codes", align_bytes=64)
+        nc.sync.dma_start(out=w2_right[:], in_=w2_rows[:, :, N // 2 :])
+        for m in (0, 32):
+            nc.scalar.copy(*deal_views(w2_right, w2_dealt, slice(m, m + 32), slice(64 + m, 96 + m)))
         far = [keep.tile([P, S], F32, name=f"far{t}") for t in range(PACK)]
         z_pairs = [keep.tile([P, 2, HALF, 2], BF16, name=f"z_pairs{i}", tag=f"z_pairs{i}") for i in range(2)]
 
@@ -128,8 +131,7 @@ def tile_picked_skipcrossbtwicp_none_p_kernel(tc, x_words, x_scales, w1, gn, w2,
             nc.scalar.activation(z_pairs[i][:, t // 2, :, t % 2], far[t][:, halves[i]], ACT.Copy, scale=gain[:, t : t + 1])
 
         for i in range(2):
-            nc.vector.tensor_tensor(st_win[0][:, halves[i]], y_win[0][:, halves[i]], st_win[0][:, S + i * HALF : S + (i + 1) * HALF], ALU.mult)
-        nc.vector.quantize_mx(out=w2_codes[:].bitcast(FP8X4), scales=w2_plane[:], in_=w2_dealt[:])
+            nc.vector.tensor_tensor(st_win[0][:, halves[i]], sigmoid0[:].indirect(n1_sb[:, list_halves[i]]), y_win[0][:, halves[i]], ALU.mult)
         for t in range(PACK - 1):
             nc.vector.tensor_copy(far[t][:], st_win[t][:].indirect(n1_sb[:]))
             gate(t + 1)
@@ -142,8 +144,7 @@ def tile_picked_skipcrossbtwicp_none_p_kernel(tc, x_words, x_scales, w1, gn, w2,
             larger(3, halves[i])
             scale(3, i)
 
-        y_far0 = st_win[3][:, S : S + HALF]
-        nc.vector.tensor_copy(y_far0, y_win[0][:].indirect(n3_sb[:, list_halves[0]]))
+        nc.vector.quantize_mx(out=w2_codes[:].bitcast(FP8X4), scales=w2_plane[:], in_=w2_dealt[:])
 
         z_woven = [keep.tile([P, PACK * HALF], BF16, name=f"z_woven{i}", tag=f"z_woven{i}", align_bytes=64) for i in range(2)]
         z_codes = keep.tile([P, S], U32, name="z_codes", align_bytes=64)
@@ -154,9 +155,8 @@ def tile_picked_skipcrossbtwicp_none_p_kernel(tc, x_words, x_scales, w1, gn, w2,
             nc.vector.tensor_copy(dst, src)
         for i in range(2):
             nc.vector.quantize_mx(out=z_codes[:, halves[i]].bitcast(FP8X4), scales=z_plane[:, halves[i]], in_=z_woven[i][:])
-        y_far1 = keep.tile([P, HALF], F32, name="y_far1", tag="z_woven1", align_bytes=64)
-        nc.vector.tensor_copy(y_far1[:], y_win[0][:].indirect(n3_sb[:, list_halves[1]]))
-        y_far = [y_far0, y_far1[:]]
+        y_far = keep.tile([P, HALF], F32, name="y_far", tag="z_woven1", align_bytes=64)
+        nc.vector.tensor_copy(y_far[:], y_win[0][:].indirect(n3_sb[:, list_halves[0]]))
 
         first = [keep.tile([P, S], F32, name=f"first{t}") for t in range(PACK)]
         h0_ps = [psum.tile([P, HALF], F32, name=f"h0_ps{i}", tag=f"bank{5 + i}") for i in range(2)]
@@ -164,19 +164,20 @@ def tile_picked_skipcrossbtwicp_none_p_kernel(tc, x_words, x_scales, w1, gn, w2,
         for i in range(2):
             product(h0_ps[i][:], w2_codes, w2_plane, 0, z_codes, z_plane, halves[i])
             nc.scalar.activation(st_win[0][:, halves[i]], h0_ps[i][:], ACT.Copy, scale=0.75)
-            nc.vector.scalar_tensor_tensor(first[0][:, halves[i]], h0_ps[i][:], -0.75, y_far[i], ALU.mult, ALU.mult)
             product(h_ps[1][:, halves[i]], w2_codes, w2_plane, 1, z_codes, z_plane, halves[i])
+        y_minus = [keep.tile([P, S], F32, name=f"y_minus{t}", tag=f"z_pairs{t}") for t in range(2)]
+        y_minus = y_minus + [keep.tile([P, S], F32, name="y_minus2", tag="z_woven0", align_bytes=64)]
+        nc.scalar.activation(y_minus[0][:], y_win[0][:, :S], ACT.Copy, scale=-1.0)
         for t in (2, 3):
             product(h_ps[t][:], w2_codes, w2_plane, t, z_codes, z_plane, slice(0, S))
 
         def leave_bank(t):
+            if t < 3:
+                nc.scalar.activation(y_minus[t][:], y_win[t][:, :S], ACT.Copy, scale=-1.0)
             nc.scalar.activation(st_win[t][:, :S], h_ps[t][:], ACT.Copy, scale=0.75)
 
         leave_bank(1)
 
-        y_minus = [None] + [keep.tile([P, S], F32, name=f"y_minus{t}", tag=f"z_pairs{t - 1}") for t in (1, 2)]
-        for t in (1, 2):
-            nc.scalar.activation(y_minus[t][:], y_win[t][:, :S], ACT.Copy, scale=-1.0)
         out_rows = out.rearrange("(p t) s -> p t s", t=PACK)
 
         def add_on_tensor(t, terms, c, banks):
@@ -193,12 +194,14 @@ def tile_picked_skipcrossbtwicp_none_p_kernel(tc, x_words, x_scales, w1, gn, w2,
             for block in blocks:
                 nc.tensor.transpose(back_ps[:, block], turned[:, block], ident[:])
             done = keep.tile([P, width], F32, name=f"done{banks[1]}")
-            nc.scalar.activation(done[:], back_ps[:], ACT.Copy, scale=-1.0 if t == 0 else 1.0)
+            nc.scalar.copy(done[:], back_ps[:])
             nc.scalar.dma_start(out=out_rows[:, t, c], in_=done[:])
 
         whole = slice(0, S)
-        nc.vector.tensor_tensor(far[0][:], st_win[0][:].indirect(n2_sb[:]), y_win[0][:, :S], ALU.mult)
-        add_on_tensor(0, (first[0], far[0]), whole, (2, 4))
+        nc.vector.tensor_tensor(first[0][:, halves[0]], y_far[:], st_win[0][:, halves[0]], ALU.mult)
+        nc.vector.tensor_tensor(far[0][:], st_win[0][:].indirect(n2_sb[:]), y_minus[0][:], ALU.mult)
+        nc.vector.tensor_tensor(first[0][:, halves[1]], y_win[0][:].indirect(n3_sb[:, list_halves[1]]), st_win[0][:, halves[1]], ALU.mult)
+        add_on_tensor(0, (far[0], first[0]), whole, (2, 4))
         leave_bank(2)
         nc.vector.tensor_tensor(far[1][:], st_win[1][:].indirect(n2_sb[:]), y_minus[1][:], ALU.mult)
         nc.vector.tensor_tensor(first[1][:], y_win[1][:].indirect(n3_sb[:]), st_win[1][:, :S], ALU.mult)

from contextlib import ExitStack

import concourse.mybir as mybir
from concourse.masks import make_identity

K, T, S, N, H = 512, 2048, 512, 512, 512
FLOPS = 2 * K * H * S + 2 * H * N * S

F32 = mybir.dt.float32
BF16 = mybir.dt.bfloat16
I32 = mybir.dt.int32
U32 = mybir.dt.uint32
U16 = mybir.dt.uint16
U8 = mybir.dt.uint8
FP8X4 = mybir.dt.float8_e4m3fn_x4
ALU = mybir.AluOpType
ACT = mybir.ActivationFunctionType

P = 128
PACK = 4


def deal_views(raw, dealt, m_raw, m_dealt):
    src = raw[:].rearrange("p j (m t) -> p m j t", t=PACK)[:, m_raw, :, :]
    dst = dealt[:].rearrange("p (t m j) -> p m j t", t=PACK, j=PACK)[:, m_dealt, :, :]
    return dst, src


def tile_picked_skipcrossbtwicp_none_p_kernel(tc, x_words, x_scales, w1, gn, w2, offs, n1, n2, n3, out):
    nc = tc.nc
    with ExitStack() as ctx:
        keep = ctx.enter_context(tc.tile_pool(name="keep", bufs=1))
        psum = ctx.enter_context(tc.psum_pool(name="psum", bufs=1))
        HALF = S // 2
        halves = [slice(0, HALF), slice(HALF, S)]
        list_halves = [slice(0, HALF // 16), slice(HALF // 16, S // 16)]

        offs_sb = keep.tile([P, S // 16], U16, name="offs_sb")
        n1_sb = keep.tile([P, S // 16], U16, name="n1_sb")
        n2_sb = keep.tile([P, S // 16], U16, name="n2_sb")
        n3_sb = keep.tile([P, S // 16], U16, name="n3_sb")
        table_words = keep.tile([P, T], U32, name="table_words", align_bytes=64)
        table_scales = keep.tile([P, T], U8, name="table_scales", tag="scales_then_codes", align_bytes=64)
        w1_raw = [keep.tile([P, PACK, H // 2], F32, name=f"w1_raw{i}", tag=f"raw{i}") for i in range(2)]
        gain = keep.tile([P, PACK], F32, name="gain")
        y_win = [keep.tile([P, 2 * S], F32, name=f"y_win{t}") for t in range(PACK)]
        st_win = [keep.tile([P, 2 * S], F32, name=f"st_win{t}") for t in range(PACK)]
        warm = keep.tile([P, 2], F32, name="warm")
        ident = keep.tile([P, P], F32, name="ident")

        nc.vector.memset(table_scales[:].bitcast(I32), 0)
        nc.vector.memset(warm[:, 0:1], 0.0)
        w1_rows = w1.rearrange("(p j) c -> p j c", j=PACK)
        nc.sync.dma_start(out=w1_raw[0][:], in_=w1_rows[:, :, : H // 2])
        for q in range(4):
            nc.sync.dma_start(out=table_scales[32 * q : 32 * q + 4, :].bitcast(I32), in_=x_scales[0, 4 * q : 4 * q + 4, :].bitcast(I32))
        nc.sync.dma_start(offs_sb[:], offs)
        nc.sync.dma_start(out=w1_raw[1][:], in_=w1_rows[:, :, H // 2 :])
        nc.sync.dma_start(out=table_words[:].bitcast(I32), in_=x_words[0].rearrange("p n t -> p (n t)").bitcast(I32))
        nc.sync.dma_start(n1_sb[:], n1)
        nc.sync.dma_start(n3_sb[:], n3)
        nc.sync.dma_start(n2_sb[:], n2)
        nc.gpsimd.dma_start(out=gain[:], in_=gn.rearrange("(p t) o -> p (t o)", t=PACK))
        nc.scalar.activation(warm[:, 1:2], warm[:, 0:1], ACT.Sigmoid)
        for t in range(PACK):
            nc.vector.memset(y_win[t][:, S:], 0.0)
        nc.vector.memset(st_win[0][:, S:], 0.0)
        sigmoid0 = keep.tile([P, S], F32, name="sigmoid0")
        make_identity(nc, ident[:])

        w1_dealt = keep.tile([P, PACK * H], BF16, name="w1_dealt", align_bytes=64)
        nc.vector.tensor_copy(*deal_views(w1_raw[0], w1_dealt, slice(0, 64), slice(0, 64)))
        nc.vector.tensor_copy(*deal_views(w1_raw[1], w1_dealt, slice(0, 32), slice(64, 96)))
        nc.scalar.copy(*deal_views(w1_raw[1], w1_dealt, slice(32, 64), slice(96, 128)))

        x_plane = keep.tile([P, S], U8, name="x_plane", align_bytes=64)
        nc.vector.tensor_copy(x_plane[:], table_scales[:].indirect(offs_sb[:]))
        w1_codes = keep.tile([P, H], U32, name="w1_codes", align_bytes=64)
        w1_plane = keep.tile([P, H], U8, name="w1_plane", align_bytes=64)
        nc.vector.quantize_mx(out=w1_codes[:].bitcast(FP8X4), scales=w1_plane[:], in_=w1_dealt[:])
        x_codes = keep.tile([P, S], U32, name="x_codes", tag="scales_then_codes", align_bytes=64)
        for i in range(2):
            nc.vector.tensor_copy(x_codes[:, halves[i]], table_words[:].indirect(offs_sb[:, list_halves[i]]))

        w2_rows = w2.rearrange("(p j) c -> p j c", j=PACK)
        w2_left = keep.tile([P, PACK, N // 2], F32, name="w2_left", tag="raw0")
        nc.sync.dma_start(out=w2_left[:], in_=w2_rows[:, :, : N // 2])

        def product(dst, w_codes, w_plane, t, codes, plane, c):
            cols = slice(t * P, (t + 1) * P)
            nc.tensor.matmul_mx(out=dst, lhsT=w_codes[:, cols].bitcast(FP8X4), lhsT_scale=w_plane[:, cols],
                                rhs=codes[:, c].bitcast(FP8X4), rhs_scale=plane[:, c], start=True, stop=True)

        y0_ps = [psum.tile([P, HALF], F32, name=f"y0_ps{i}", tag=f"bank{i}") for i in range(2)]
        y_ps = {1: psum.tile([P, S], F32, name="y_ps1", tag="bank2")}
        for i in range(2):
            product(y0_ps[i][:], w1_codes, w1_plane, 0, x_codes, x_plane, halves[i])
            nc.scalar.activation(sigmoid0[:, halves[i]], y0_ps[i][:], ACT.Sigmoid)
            nc.scalar.copy(y_win[0][:, halves[i]], y0_ps[i][:])
            product(y_ps[1][:, halves[i]], w1_codes, w1_plane, 1, x_codes, x_plane, halves[i])

        def sig(t):
            nc.scalar.activation(st_win[t][:, S:], y_win[t][:].indirect(n1_sb[:]), ACT.Sigmoid)

        w2_dealt = keep.tile([P, PACK * N], BF16, name="w2_dealt", align_bytes=64)
        w2_codes = keep.tile([P, N], U32, name="w2_codes", align_bytes=64)
        w2_plane = keep.tile([P, N], U8, name="w2_plane", align_bytes=64)
        nc.vector.tensor_copy(*deal_views(w2_left, w2_dealt, slice(0, 64), slice(0, 64)))
        nc.vector.tensor_copy(y_win[1][:, :S], y_ps[1][:])
        sig(1)
        for t in (2, 3):
            y_ps.setdefault(t, psum.tile([P, S], F32, name=f"y_ps{t}", tag=f"bank{t - 1}"))
            product(y_ps[t][:], w1_codes, w1_plane, t, x_codes, x_plane, slice(0, S))
            nc.scalar.copy(y_win[t][:, :S], y_ps[t][:])
            sig(t)

        w2_right = keep.tile([P, PACK, N // 2], F32, name="w2_right", tag="scales_then_codes", align_bytes=64)
        nc.sync.dma_start(out=w2_right[:], in_=w2_rows[:, :, N // 2 :])
        for m in (0, 32):
            nc.scalar.copy(*deal_views(w2_right, w2_dealt, slice(m, m + 32), slice(64 + m, 96 + m)))
        far = [keep.tile([P, S], F32, name=f"far{t}") for t in range(PACK)]
        z_pairs = [keep.tile([P, 2, HALF, 2], BF16, name=f"z_pairs{i}", tag=f"z_pairs{i}") for i in range(2)]

        def gate(t):
            nc.vector.tensor_tensor(st_win[t][:, :S], y_win[t][:, :S], st_win[t][:, S:], ALU.mult)

        def larger(t, c):
            nc.vector.tensor_tensor(far[t][:, c], far[t][:, c], st_win[t][:, c], ALU.max)

        def scale(t, i):
            nc.scalar.activation(z_pairs[i][:, t // 2, :, t % 2], far[t][:, halves[i]], ACT.Copy, scale=gain[:, t : t + 1])

        for i in range(2):
            nc.vector.tensor_tensor(st_win[0][:, halves[i]], sigmoid0[:].indirect(n1_sb[:, list_halves[i]]), y_win[0][:, halves[i]], ALU.mult)
        for t in range(PACK - 1):
            nc.vector.tensor_copy(far[t][:], st_win[t][:].indirect(n1_sb[:]))
            gate(t + 1)
            larger(t, slice(0, S))
            for i in range(2):
                scale(t, i)
        for i in range(2):
            nc.vector.tensor_copy(far[3][:, halves[i]], st_win[3][:].indirect(n1_sb[:, list_halves[i]]))
        for i in range(2):
            larger(3, halves[i])
            scale(3, i)

        nc.vector.quantize_mx(out=w2_codes[:].bitcast(FP8X4), scales=w2_plane[:], in_=w2_dealt[:])

        z_woven = [keep.tile([P, PACK * HALF], BF16, name=f"z_woven{i}", tag=f"z_woven{i}", align_bytes=64) for i in range(2)]
        z_codes = keep.tile([P, S], U32, name="z_codes", align_bytes=64)
        z_plane = keep.tile([P, S], U8, name="z_plane", align_bytes=64)
        for i in range(2):
            src = z_pairs[i][:].rearrange("p u s e -> p (u s e)").bitcast(F32).rearrange("p (u s) -> p s u", u=2)
            dst = z_woven[i][:].bitcast(F32).rearrange("p (s u) -> p s u", u=2)
            nc.vector.tensor_copy(dst, src)
        for i in range(2):
            nc.vector.quantize_mx(out=z_codes[:, halves[i]].bitcast(FP8X4), scales=z_plane[:, halves[i]], in_=z_woven[i][:])
        y_far = keep.tile([P, HALF], F32, name="y_far", tag="z_woven1", align_bytes=64)
        nc.vector.tensor_copy(y_far[:], y_win[0][:].indirect(n3_sb[:, list_halves[0]]))

        first = [keep.tile([P, S], F32, name=f"first{t}") for t in range(PACK)]
        h0_ps = [psum.tile([P, HALF], F32, name=f"h0_ps{i}", tag=f"bank{5 + i}") for i in range(2)]
        h_ps = [None] + [psum.tile([P, S], F32, name=f"h_ps{t}", tag=f"bank{(6 + t) % 8}") for t in range(1, PACK)]
        for i in range(2):
            product(h0_ps[i][:], w2_codes, w2_plane, 0, z_codes, z_plane, halves[i])
            nc.scalar.activation(st_win[0][:, halves[i]], h0_ps[i][:], ACT.Copy, scale=0.75)
            product(h_ps[1][:, halves[i]], w2_codes, w2_plane, 1, z_codes, z_plane, halves[i])
        y_minus = [keep.tile([P, S], F32, name=f"y_minus{t}", tag=f"z_pairs{t}") for t in range(2)]
        y_minus = y_minus + [keep.tile([P, S], F32, name="y_minus2", tag="z_woven0", align_bytes=64)]
        nc.scalar.activation(y_minus[0][:], y_win[0][:, :S], ACT.Copy, scale=-1.0)
        for t in (2, 3):
            product(h_ps[t][:], w2_codes, w2_plane, t, z_codes, z_plane, slice(0, S))

        def leave_bank(t):
            if t < 3:
                nc.scalar.activation(y_minus[t][:], y_win[t][:, :S], ACT.Copy, scale=-1.0)
            nc.scalar.activation(st_win[t][:, :S], h_ps[t][:], ACT.Copy, scale=0.75)

        leave_bank(1)

        out_rows = out.rearrange("(p t) s -> p t s", t=PACK)

        def add_on_tensor(t, terms, c, banks):
            width = c.stop - c.start
            blocks = [slice(b * P, (b + 1) * P) for b in range(width // P)]
            turned_ps = psum.tile([P, width], F32, name=f"turned_ps{banks[1]}", tag=f"bank{banks[0]}")
            for k, term in enumerate(terms):
                for b, block in enumerate(blocks):
                    nc.tensor.matmul(turned_ps[:, block], lhsT=term[:, c][:, block], rhs=ident[:], is_transpose=True,
                                     start=(k == 0 and b == 0), stop=(k == 1 and b == len(blocks) - 1))
            turned = keep.tile([P, width], F32, name=f"turned{banks[1]}")
            nc.scalar.copy(turned[:], turned_ps[:])
            back_ps = psum.tile([P, width], F32, name=f"back_ps{banks[1]}", tag=f"bank{banks[1]}")
            for block in blocks:
                nc.tensor.transpose(back_ps[:, block], turned[:, block], ident[:])
            done = keep.tile([P, width], F32, name=f"done{banks[1]}")
            nc.scalar.copy(done[:], back_ps[:])
            nc.scalar.dma_start(out=out_rows[:, t, c], in_=done[:])

        whole = slice(0, S)
        nc.vector.tensor_tensor(first[0][:, halves[0]], y_far[:], st_win[0][:, halves[0]], ALU.mult)
        nc.vector.tensor_tensor(far[0][:], st_win[0][:].indirect(n2_sb[:]), y_minus[0][:], ALU.mult)
        nc.vector.tensor_tensor(first[0][:, halves[1]], y_win[0][:].indirect(n3_sb[:, list_halves[1]]), st_win[0][:, halves[1]], ALU.mult)
        add_on_tensor(0, (far[0], first[0]), whole, (2, 4))
        leave_bank(2)
        nc.vector.tensor_tensor(far[1][:], st_win[1][:].indirect(n2_sb[:]), y_minus[1][:], ALU.mult)
        nc.vector.tensor_tensor(first[1][:], y_win[1][:].indirect(n3_sb[:]), st_win[1][:, :S], ALU.mult)
        add_on_tensor(1, (far[1], first[1]), whole, (2, 6))
        leave_bank(3)
        nc.vector.tensor_tensor(far[2][:], st_win[2][:].indirect(n2_sb[:]), y_minus[2][:], ALU.mult)
        for i in range(2):
            nc.vector.tensor_tensor(first[2][:, halves[i]], y_win[2][:].indirect(n3_sb[:, list_halves[i]]), st_win[2][:, halves[i]], ALU.mult)
        add_on_tensor(2, (far[2], first[2]), halves[0], (2, 7))
        nc.vector.tensor_tensor(first[3][:], y_win[3][:].indirect(n3_sb[:]), st_win[3][:, :S], ALU.mult)
        nc.vector.tensor_tensor(first[2][:, halves[1]], first[2][:, halves[1]], far[2][:, halves[1]], ALU.add)
        nc.sync.dma_start(out=out_rows[:, 2, halves[1]], in_=first[2][:, halves[1]])
        for i in range(2):
            nc.vector.tensor_tensor(far[3][:, halves[i]], st_win[3][:].indirect(n2_sb[:, list_halves[i]]), y_win[3][:, halves[i]], ALU.mult)
        for c in halves:
            nc.vector.tensor_tensor(first[3][:, c], first[3][:, c], far[3][:, c], ALU.subtract)
            nc.sync.dma_start(out=out_rows[:, 3, c], in_=first[3][:, c])
